import numpy as np
import ml_dtypes


def mxq(x, axis, fmt="e4m3"):
    dtype, down = {"e4m3": (ml_dtypes.float8_e4m3fn, 7), "e5m2": (ml_dtypes.float8_e5m2, 14)}[fmt]
    v = np.moveaxis(np.asarray(x, np.float32).astype(ml_dtypes.bfloat16).astype(np.float64), axis, -1)
    blocks = v.reshape(v.shape[:-1] + (-1, 32))
    amax = np.abs(blocks).max(-1, keepdims=True)
    byte = np.maximum(np.where(amax > 0, np.frexp(amax)[1] - 1 + 127, 0) - down, 1)
    scale = np.exp2(byte - 127.0)
    codes = (blocks / scale).astype(np.float32).astype(dtype).astype(np.float64)
    return np.moveaxis((codes * scale).reshape(v.shape), -1, axis)


WIDE = False


def mx_kscale(k):
    if not WIDE:
        return np.ones(k)
    levels = np.array([10, -10, 5, -5, 0])
    if k % 512:
        return np.exp2(np.random.permutation(np.resize(levels, k // 32))).repeat(32)
    a = np.empty((k // 512, 16))
    for p in range(k // 512):
        a[p, :8] = np.random.permutation(np.resize(levels, 8))
        for g in range(8):
            far = levels[np.abs(levels - a[p, g]) >= 10]
            a[p, g + 8] = far[np.random.randint(len(far))]
    return np.exp2(a.ravel()).repeat(32)


def f64(x):
    return np.asarray(x).astype(np.float64)


def striped(idx):
    return np.tile(np.asarray(idx).reshape(-1, 16).T, (8, 1)).astype(np.uint16)


def unstriped(offs):
    return offs[:16].T.reshape(-1).astype(np.int64)


E2M1 = np.array([0.0, 0.5, 1.0, 1.5, 2.0, 3.0, 4.0, 6.0, -0.0, -0.5, -1.0, -1.5, -2.0, -3.0, -4.0, -6.0])


def pack_weight(w, fmt):
    k, n = w.shape
    w = f64(np.asarray(w, np.float32).astype(ml_dtypes.bfloat16)).reshape(k // 32, 32, n)
    amax = np.abs(w).max(1)
    if fmt == "e4m3":
        byte = np.frexp(amax)[1] - 1 + 127 - 7
    else:
        mant, ex = np.frexp(amax / 6.0)
        byte = np.where(mant > 0.5, ex, ex - 1) + 127
    byte = np.clip(np.where(amax > 0, byte, 1), 1, 254)
    scaled = (w * np.exp2(127.0 - byte)[:, None, :]).reshape(k, n).astype(np.float32)
    by_word = np.ascontiguousarray(scaled.reshape(k // 512, 128, 4, n).transpose(0, 1, 3, 2))
    if fmt == "e4m3":
        words = by_word.astype(ml_dtypes.float8_e4m3fn).view(np.uint8)
    else:
        c = by_word.astype(ml_dtypes.float4_e2m1fn).view(np.uint8) & 0xF
        words = (c[..., 0::2] | (c[..., 1::2] << 4)).reshape(k // 512, 128, 2 * n)
    return np.ascontiguousarray(words), np.ascontiguousarray(byte.astype(np.uint8).reshape(k // 512, 16, n))


def unpack_weight(words, scales, fmt):
    g, _, n = scales.shape
    words = np.ascontiguousarray(words).reshape(g, 128, n, -1)
    if fmt == "e4m3":
        vals = words.view(ml_dtypes.float8_e4m3fn).astype(np.float64)
    else:
        nib = np.empty((g, 128, n, 4), np.uint8)
        nib[..., 0::2] = words & 0xF
        nib[..., 1::2] = words >> 4
        vals = E2M1[nib]
    vals = vals * np.repeat(np.exp2(scales.astype(np.float64) - 127.0), 8, axis=1)[..., None]
    return vals.transpose(0, 1, 3, 2).reshape(g * 512, n)


def bf(x):
    return np.asarray(x, np.float32).astype(ml_dtypes.bfloat16)


def planes(Y):
    r, m = Y.shape
    b = f64(bf(Y)).reshape(r // 32, 32, m)
    amax = np.abs(b).max(1)
    byte = np.clip(np.where(amax > 0, np.frexp(amax)[1] - 1 + 127 - 7, 1), 1, 254)
    codes = (b * np.exp2(127.0 - byte)[:, None, :]).reshape(r, m).astype(np.float32).astype(ml_dtypes.float8_e4m3fn).view(np.uint8)
    words = codes.reshape(r // 512, 128, 4, m).transpose(0, 1, 3, 2)
    return np.ascontiguousarray(words), np.ascontiguousarray(byte.astype(np.uint8).reshape(r // 512, 16, m))


D, T, I, Q, E, U, M, C = 512, 2048, 512, 256, 512, 1024, 1024, 512


def setup_inputs():
    n = np.random.standard_normal
    idx = np.random.permutation(T)[:I]
    idx2 = np.random.permutation(U)[:I]
    idx3 = np.random.permutation(M)[:Q]
    fd = mx_kscale(D)
    fi = mx_kscale(I)
    fc = mx_kscale(C)
    ti = np.ones(T)
    ti[idx] = fi
    keysp = pack_weight(n((D, T)) / fd[:, None], "e2m1")
    return {
        "query": (n((D, Q)) * 0.9 / np.sqrt(D) * fd[:, None]).astype(np.float32),
        "keys_words": keysp[0],
        "keys_scales": keysp[1],
        "query2": (n((D, Q)) * 0.9 / np.sqrt(D) * fd[:, None]).astype(np.float32),
        "notes": (n((D, U)) / fd[:, None]).astype(np.float32),
        "lam": (np.random.uniform(0.1, 0.5, (Q, 1))).astype(np.float32),
        "os": (np.random.uniform(0.02, 0.08, (1, I)) * fi).astype(np.float32),
        "vals": (n((E, T)) / ti).astype(np.float32),
        "wm": (n((C, E)) * 1.0 / np.sqrt(C) * fc[:, None]).astype(np.float32),
        "mstore": (n((C, M)) / fc[:, None]).astype(np.float32),
        "offs": striped(idx),
        "offs2": striped(idx2),
        "offs3": striped(idx3),
    }


def reference(query, keys_words, keys_scales, query2, notes, lam, os, vals, wm, mstore, offs, offs2, offs3):
    idx = unstriped(offs)
    idx2 = unstriped(offs2)
    idx3 = unstriped(offs3)
    keysu = unpack_weight(keys_words, keys_scales, "e2m1")
    queryq = mxq(f64(query), 0, "e4m3")
    keysidxg = keysu[:, idx]
    a = queryq.T @ keysidxg
    query2q = mxq(f64(query2), 0, "e4m3")
    notesidx2q = mxq(f64(notes)[:, idx2], 0, "e4m3")
    b = query2q.T @ notesidx2q
    s = np.maximum(a, b) + np.minimum(a, b) * f64(lam)
    w = np.maximum(s, 0.0)
    wo1 = w * f64(os)
    wt1 = wo1.T
    vt1 = f64(vals)[:, idx].T
    vt1q = mxq(vt1, 0, "e4m3")
    wt1q = mxq(wt1, 0, "e4m3")
    o = vt1q.T @ wt1q
    wmq = mxq(f64(wm), 0, "e4m3")
    mstoreq = mxq(f64(mstore), 0, "e4m3")
    me = wmq.T @ mstoreq
    y = o * me[:, idx3]
    words, scales = planes(y)
    return y, words, scales

@@ -1,0 +1,230 @@
+from contextlib import ExitStack
+
+import concourse.mybir as mybir
+from concourse.masks import make_identity
+
+D, T, I, Q, E, U, M, C = 512, 2048, 512, 256, 512, 1024, 1024, 512
+FLOPS = 2 * (2 * D * Q * I + I * E * Q + C * E * M)
+
+F32 = mybir.dt.float32
+BF16 = mybir.dt.bfloat16
+I32 = mybir.dt.int32
+U32 = mybir.dt.uint32
+U16 = mybir.dt.uint16
+U8 = mybir.dt.uint8
+FP8X4 = mybir.dt.float8_e4m3fn_x4
+FP4X4 = mybir.dt.float4_e2m1fn_x4
+ALU = mybir.AluOpType
+COPY = mybir.ActivationFunctionType.Copy
+
+P = 128
+PACK = 4
+BANK = 512
+
+
+def tile_attend_twopools_remembered_lean_pl_kernel(
+    tc, query, keys_words, keys_scales, query2, notes, lam, slot_factor, vals, wm, mstore,
+    offs, offs2, offs3, out_0, out_1, out_2,
+):
+    nc = tc.nc
+    with ExitStack() as ctx:
+        sb = ctx.enter_context(tc.tile_pool(name="sb", bufs=1))
+        ps = ctx.enter_context(tc.psum_pool(name="ps", bufs=1))
+
+        def tile(name, shape, dtype, tag=""):
+            return sb.tile(shape, dtype, name=name, tag=tag, align_bytes=64)
+
+        def load(name, shape, dtype, src, queue=nc.sync, tag=""):
+            t = tile(name, shape, dtype, tag)
+            queue.dma_start(out=t[:], in_=src)
+            return t
+
+        def copy(engine, out, in_):
+            if engine is nc.vector:
+                nc.vector.tensor_copy(out=out, in_=in_)
+            else:
+                nc.scalar.copy(out=out, in_=in_)
+
+        def weave(engine, name, planes, width, tag=""):
+            woven = tile(name, [P, width * PACK], BF16, tag)
+            copy(
+                engine,
+                woven[:].rearrange("p (c i t) -> p c t i", i=4, t=PACK),
+                planes.rearrange("p t (c i) -> p c t i", i=4),
+            )
+            return woven
+
+        def quantise(name, woven, width):
+            codes = tile(name + "_codes", [P, width], U32)
+            scales = tile(name + "_scales", [P, width], U8)
+            nc.vector.quantize_mx(out=codes[:].bitcast(FP8X4), scales=scales[:], in_=woven)
+            return codes, scales
+
+        def product(out, left, cols, right, right_dtype):
+            nc.tensor.matmul_mx(
+                out=out, lhsT=left[0][:, cols].bitcast(FP8X4), lhsT_scale=left[1][:, cols],
+                rhs=right[0][:].bitcast(right_dtype), rhs_scale=right[1][:], start=True, stop=True,
+            )
+
+        def gather(engine, out, window, offsets):
+            if engine is nc.vector:
+                nc.vector.tensor_copy(out=out, in_=window[:].indirect(offsets))
+            else:
+                nc.scalar.activation(out=out, in_=window[:].indirect(offsets), func=COPY)
+
+        def gather_shared(out, window, offsets, n):
+            gather(nc.scalar, out[:, 0 : n // 2], window, offsets[:, 0 : n // 32])
+            gather(nc.vector, out[:, n // 2 : n], window, offsets[:, n // 32 : n // 16])
+
+        key_scales = tile("key_scales", [P, T], U8)
+        nc.vector.memset(key_scales[:].bitcast(U32), 0)
+        identity = tile("identity", [P, P], F32)
+        make_identity(nc, identity[:])
+
+        by_plane = "(p t) n -> p t n"
+        notes_planes = notes.rearrange(by_plane, t=PACK)
+        vals_planes = vals.rearrange(by_plane, t=PACK)
+        mstore_planes = mstore.rearrange(by_plane, t=PACK)
+        ms_raw, notes_raw, vals_raw = {}, {}, {}
+        wm_raw = load("wm_raw", [P, PACK, E], F32, wm.rearrange(by_plane, t=PACK))
+        for quad in range(4):
+            nc.sync.dma_start(
+                out=key_scales[32 * quad : 32 * quad + 4, :].bitcast(I32),
+                in_=keys_scales[0][4 * quad : 4 * quad + 4, :].bitcast(I32),
+            )
+        ms_raw[0] = load("ms_raw0", [P, PACK, BANK], F32, mstore_planes[:, :, 0:BANK])
+        note_list = load("note_list", [P, I // 16], U16, offs2)
+        notes_raw[0] = load("notes_raw0", [P, U], F32, notes_planes[:, 0, :])
+        key_words = tile("key_words", [P, T], U16)
+        nc.sync.dma_start(out=key_words[:].bitcast(I32), in_=keys_words[0].bitcast(I32))
+        token_list = load("token_list", [P, I // 16], U16, offs)
+        ms_raw[1] = load("ms_raw1", [P, PACK, BANK], F32, mstore_planes[:, :, BANK:M])
+        notes_raw[1] = load("notes_raw1", [P, U], F32, notes_planes[:, 1, :])
+        q_raw = load("q_raw", [P, PACK, Q], F32, query.rearrange(by_plane, t=PACK))
+        memory_list = load("memory_list", [P, Q // 16], U16, offs3)
+        notes_raw[2] = load("notes_raw2", [P, U], F32, notes_planes[:, 2, :])
+        notes_raw[3] = load("notes_raw3", [P, U], F32, notes_planes[:, 3, :])
+        q2_raw = load("q2_raw", [P, PACK, Q], F32, query2.rearrange(by_plane, t=PACK))
+        with nc.allow_non_contiguous_dma(reason="one factor to a partition"):
+            lam_col = [load("lam%d" % h, [P, 1], F32, lam[h * P : (h + 1) * P, :], queue=nc.sync) for h in range(2)]
+        factor = load("factor", [P, PACK], F32, slot_factor.rearrange("o (s r) -> (o s) r", r=PACK), queue=nc.sync)
+        vals_raw[0] = load("vals_raw0", [P, T], F32, vals_planes[:, 0, :])
+        vals_raw[1] = load("vals_raw1", [P, T], F32, vals_planes[:, 1, :])
+        vals_raw[2] = load("vals_raw2", [P, T], F32, vals_planes[:, 2, :], tag="v2")
+        vals_raw[3] = load("vals_raw3", [P, T], F32, vals_planes[:, 3, :], tag="v3")
+
+        def wide_bank(name, tag):
+            return ps.tile([P, BANK], F32, name=name, tag=tag, bufs=4)
+
+        memory = [tile("memory%d" % t, [P, M], F32) for t in range(PACK)]
+        notes_picked = tile("notes_picked", [P, PACK, I], BF16)
+        weights = tile("weights", [P, Q * PACK], BF16)
+        dealt = "p (s r) -> p r s"
+        out_planes = out_0.rearrange(by_plane, t=PACK)
+
+        def memories(half, ms_q):
+            for t in range(PACK):
+                bank = wide_bank("me_ps", "other")
+                product(bank[:], wm_q, slice(t * P, (t + 1) * P), ms_q, FP8X4)
+                nc.scalar.copy(out=memory[t][:, half * BANK : (half + 1) * BANK], in_=bank[:])
+
+        def token_scores(h):
+            a = wide_bank("a_ps", "score")
+            product(a[:], q_q, slice(h * P, (h + 1) * P), keys, FP4X4)
+            a_sb = tile("a_sb%d" % h, [P, PACK, P], F32)
+            nc.scalar.copy(out=a_sb[:], in_=a[:].rearrange(dealt, r=PACK))
+            return a_sb
+
+        def scores(h):
+            b = wide_bank("b_ps", "score")
+            product(b[:], q2_q, slice(h * P, (h + 1) * P), notes_q, FP8X4)
+            larger = tile("larger%d" % h, [P, PACK, P], F32)
+            smaller = tile("smaller%d" % h, [P, PACK, P], F32)
+            nc.vector.tensor_tensor(out=larger[:], in0=b[:].rearrange(dealt, r=PACK), in1=a_sb[h][:], op=ALU.max)
+            nc.vector.tensor_tensor(out=smaller[:], in0=b[:].rearrange(dealt, r=PACK), in1=a_sb[h][:], op=ALU.min)
+            score = tile("score%d" % h, [P, PACK, P], F32)
+            nc.vector.scalar_tensor_tensor(
+                out=score[:], in0=smaller[:], scalar=lam_col[h][:], in1=larger[:], op0=ALU.mult, op1=ALU.add
+            )
+            turned = wide_bank("turned_ps", "score")
+            for r in range(PACK):
+                nc.tensor.transpose(turned[:, r * P : (r + 1) * P], score[:, r, :], identity[:])
+            nc.vector.scalar_tensor_tensor(
+                out=weights[:, h * BANK : (h + 1) * BANK].rearrange("p (q r) -> p q r", r=PACK),
+                in0=turned[:].rearrange("p (r q) -> p q r", r=PACK),
+                scalar=0.0,
+                in1=factor[:].unsqueeze(1).to_broadcast([P, P, PACK]),
+                op0=ALU.max,
+                op1=ALU.mult,
+            )
+
+        def pick_values(t, engine):
+            picked = tile("vals_picked%d" % t, [P, I], BF16)
+            if engine is None:
+                gather_shared(picked, vals_raw[t], token_list, I)
+            else:
+                gather(engine, picked[:], vals_raw[t], token_list[:])
+            return picked
+
+        def turn_values(t0, picked, engine, bank, words):
+            n = len(picked)
+            pairs_ps = bank[:, 0 : n * 2 * P].rearrange("p (k u e) -> p k u e", k=n, u=2)
+            for k in range(n):
+                pairs = picked[k][:].bitcast(F32)
+                for u in range(2):
+                    nc.tensor.transpose(pairs_ps[:, k, u, :], pairs[:, u : I // 2 : 2], identity[:])
+            copy(
+                engine,
+                words.rearrange("p (k e u) -> p k e u", k=n, u=2),
+                pairs_ps.rearrange("p k u e -> p k e u"),
+            )
+            return quantise("v%d" % t0, words.bitcast(BF16), n * P)
+
+        def result(t0, n, v_q, bank):
+            o = bank[:, 0 : n * Q].rearrange("p (k q) -> p k q", k=n)
+            for k in range(n):
+                product(o[:, k, :], v_q, slice(k * P, (k + 1) * P), w_q, FP8X4)
+            nc.vector.tensor_tensor(out=y[:, t0 : t0 + n, :], in0=o, in1=recalled[:, t0 : t0 + n, :], op=ALU.mult)
+            nc.sync.dma_start(out=out_planes[:, t0 : t0 + n, :], in_=y[:, t0 : t0 + n, :])
+
+        wm_woven = tile("wm_woven", [P, E * PACK], BF16)
+        copy(nc.vector, wm_woven[:].rearrange("p (t m j) -> p m j t", t=PACK, j=PACK), wm_raw[:].rearrange("p j (m t) -> p m j t", t=PACK))
+        wm_q = quantise("wm", wm_woven[:], E)
+        memories(0, quantise("ms0", weave(nc.vector, "ms_woven0", ms_raw[0][:], BANK)[:], BANK))
+        gather(nc.scalar, notes_picked[:, 0, :], notes_raw[0], note_list[:])
+        keys = tile("keys", [P, I], U16), tile("keys_sc", [P, I], U8)
+        gather(nc.vector, keys[0][:], key_words, token_list[:])
+        gather(nc.vector, keys[1][:], key_scales, token_list[:])
+        memories(1, quantise("ms1", weave(nc.vector, "ms_woven1", ms_raw[1][:], BANK)[:], BANK))
+        gather(nc.scalar, notes_picked[:, 1, :], notes_raw[1], note_list[:])
+        q_q = quantise("q", weave(nc.vector, "q_woven", q_raw[:], Q)[:], Q)
+        a_sb = [token_scores(h) for h in range(2)]
+        gather(nc.vector, notes_picked[:, 2, :], notes_raw[2], note_list[:])
+        gather(nc.vector, notes_picked[:, 3, :], notes_raw[3], note_list[:])
+        notes_q = quantise("notes", weave(nc.vector, "notes_woven", notes_picked[:], I)[:], I)
+        q2_q = quantise("q2", weave(nc.vector, "q2_woven", q2_raw[:], Q)[:], Q)
+        recalled = tile("recalled", [P, PACK, Q], F32, "")
+        for t in range(PACK):
+            gather(nc.scalar, recalled[:, t, :], memory[t], memory_list[:])
+        scores(0)
+        scores(1)
+        w_q = quantise("w", weights[:], Q)
+        y_flat = tile("y", [P, PACK * Q], F32)
+        y = y_flat[:].rearrange("p (t q) -> p t q", t=PACK)
+        picked = [pick_values(t, nc.scalar) for t in range(PACK)]
+        v0 = turn_values(0, picked[0:1], nc.scalar, wide_bank("pairs_ps", "other"), tile("v_words0", [P, 2 * P], F32, "v2")[:])
+        v12 = turn_values(1, picked[1:3], nc.scalar, wide_bank("pairs_ps", "other"), tile("v_words12", [P, 4 * P], F32, "v3")[:])
+        last_bank = wide_bank("last_ps", "other")
+        v3 = turn_values(3, picked[3:4], nc.scalar, last_bank, y_flat[:, P : 3 * P])
+        result(0, 1, v0, wide_bank("o_ps", "other"))
+        result(1, 2, v12, last_bank)
+        result(3, 1, v3, wide_bank("o_ps", "other"))
+
+        y_codes, y_scales = quantise("y", weave(nc.vector, "y_woven", y[:], Q)[:], Q)
+        nc.sync.dma_start(out=out_1[0].rearrange("p n t -> p (n t)").bitcast(I32), in_=y_codes[:].bitcast(I32))
+        for quad in range(4):
+            queue = nc.sync if quad < 2 else nc.scalar
+            queue.dma_start(
+                out=out_2[0][4 * quad : 4 * quad + 4, :].bitcast(I32),
+                in_=y_scales[32 * quad : 32 * quad + 4, :].bitcast(I32),
+            )

@@ -20,6 +20,9 @@ COPY = mybir.ActivationFunctionType.Copy
 P = 128
 PACK = 4
 BANK = 512
+BANKS = 8
+PER_COLUMN = 16
+LAST_SHARE = 352
 
 
 def tile_attend_twopools_remembered_lean_pl_kernel(
@@ -31,11 +34,17 @@ def tile_attend_twopools_remembered_lean_pl_kernel(
         sb = ctx.enter_context(tc.tile_pool(name="sb", bufs=1))
         ps = ctx.enter_context(tc.psum_pool(name="ps", bufs=1))
 
-        def tile(name, shape, dtype, tag=""):
-            return sb.tile(shape, dtype, name=name, tag=tag, align_bytes=64)
+        def tile(name, shape, dtype, tag="", bufs=None):
+            return sb.tile(shape, dtype, name=name, tag=tag, bufs=bufs, align_bytes=64)
 
-        def load(name, shape, dtype, src, queue=nc.sync, tag=""):
-            t = tile(name, shape, dtype, tag)
+        def late_tile(name, shape, dtype):
+            return tile(name, shape, dtype, "late", 6)
+
+        def bank(name):
+            return ps.tile([P, BANK], F32, name=name, tag="bank", bufs=BANKS)
+
+        def load(name, shape, dtype, src, queue=nc.sync):
+            t = tile(name, shape, dtype)
             queue.dma_start(out=t[:], in_=src)
             return t
 
@@ -45,36 +54,34 @@ def tile_attend_twopools_remembered_lean_pl_kernel(
             else:
                 nc.scalar.copy(out=out, in_=in_)
 
-        def weave(engine, name, planes, width, tag=""):
-            woven = tile(name, [P, width * PACK], BF16, tag)
-            copy(
-                engine,
-                woven[:].rearrange("p (c i t) -> p c t i", i=4, t=PACK),
-                planes.rearrange("p t (c i) -> p c t i", i=4),
-            )
-            return woven
-
-        def quantise(name, woven, width):
-            codes = tile(name + "_codes", [P, width], U32)
-            scales = tile(name + "_scales", [P, width], U8)
-            nc.vector.quantize_mx(out=codes[:].bitcast(FP8X4), scales=scales[:], in_=woven)
-            return codes, scales
-
-        def product(out, left, cols, right, right_dtype):
-            nc.tensor.matmul_mx(
-                out=out, lhsT=left[0][:, cols].bitcast(FP8X4), lhsT_scale=left[1][:, cols],
-                rhs=right[0][:].bitcast(right_dtype), rhs_scale=right[1][:], start=True, stop=True,
-            )
-
         def gather(engine, out, window, offsets):
             if engine is nc.vector:
                 nc.vector.tensor_copy(out=out, in_=window[:].indirect(offsets))
             else:
                 nc.scalar.activation(out=out, in_=window[:].indirect(offsets), func=COPY)
 
-        def gather_shared(out, window, offsets, n):
-            gather(nc.scalar, out[:, 0 : n // 2], window, offsets[:, 0 : n // 32])
-            gather(nc.vector, out[:, n // 2 : n], window, offsets[:, n // 32 : n // 16])
+        def weave(engine, name, planes, width):
+            woven = tile(name, [P, width * PACK], BF16)
+            copy(
+                engine,
+                woven[:].rearrange("p (c i t) -> p c t i", i=4, t=PACK),
+                planes.rearrange("p t (c i) -> p c t i", i=4),
+            )
+            return woven[:]
+
+        def quantise(name, woven, tag="", bufs=None):
+            width = woven.shape[1] // PACK
+            codes = tile(name + "_codes", [P, width], U32, tag, bufs)
+            scales = tile(name + "_scales", [P, width], U8)
+            nc.vector.quantize_mx(out=codes[:].bitcast(FP8X4), scales=scales[:], in_=woven)
+            return codes[:], scales[:]
+
+        def product(out, left, block, right, right_dtype=FP8X4):
+            cols = slice(block * P, (block + 1) * P)
+            nc.tensor.matmul_mx(
+                out=out, lhsT=left[0][:, cols].bitcast(FP8X4), lhsT_scale=left[1][:, cols],
+                rhs=right[0].bitcast(right_dtype), rhs_scale=right[1], start=True, stop=True,
+            )
 
         key_scales = tile("key_scales", [P, T], U8)
         nc.vector.memset(key_scales[:].bitcast(U32), 0)
@@ -85,68 +92,68 @@ def tile_attend_twopools_remembered_lean_pl_kernel(
         notes_planes = notes.rearrange(by_plane, t=PACK)
         vals_planes = vals.rearrange(by_plane, t=PACK)
         mstore_planes = mstore.rearrange(by_plane, t=PACK)
-        ms_raw, notes_raw, vals_raw = {}, {}, {}
-        wm_raw = load("wm_raw", [P, PACK, E], F32, wm.rearrange(by_plane, t=PACK))
+        out_planes = out_0.rearrange(by_plane, t=PACK)
+
+        key_words = tile("key_words", [P, T], U16)
+        nc.sync.dma_start(out=key_words[:].bitcast(I32), in_=keys_words[0].bitcast(I32))
+        token_list = load("token_list", [P, I // PER_COLUMN], U16, offs)
         for quad in range(4):
             nc.sync.dma_start(
                 out=key_scales[32 * quad : 32 * quad + 4, :].bitcast(I32),
                 in_=keys_scales[0][4 * quad : 4 * quad + 4, :].bitcast(I32),
             )
-        ms_raw[0] = load("ms_raw0", [P, PACK, BANK], F32, mstore_planes[:, :, 0:BANK])
-        note_list = load("note_list", [P, I // 16], U16, offs2)
-        notes_raw[0] = load("notes_raw0", [P, U], F32, notes_planes[:, 0, :])
-        key_words = tile("key_words", [P, T], U16)
-        nc.sync.dma_start(out=key_words[:].bitcast(I32), in_=keys_words[0].bitcast(I32))
-        token_list = load("token_list", [P, I // 16], U16, offs)
-        ms_raw[1] = load("ms_raw1", [P, PACK, BANK], F32, mstore_planes[:, :, BANK:M])
-        notes_raw[1] = load("notes_raw1", [P, U], F32, notes_planes[:, 1, :])
+        wm_raw = load("wm_raw", [P, PACK, E], F32, wm.rearrange(by_plane, t=PACK))
+        note_list = load("note_list", [P, I // PER_COLUMN], U16, offs2)
+        ms_raw = [load("ms_raw0", [P, PACK, BANK], F32, mstore_planes[:, :, 0:BANK])]
+        notes_raw = [load("notes_raw0", [P, U], F32, notes_planes[:, 0, :])]
         q_raw = load("q_raw", [P, PACK, Q], F32, query.rearrange(by_plane, t=PACK))
-        memory_list = load("memory_list", [P, Q // 16], U16, offs3)
-        notes_raw[2] = load("notes_raw2", [P, U], F32, notes_planes[:, 2, :])
-        notes_raw[3] = load("notes_raw3", [P, U], F32, notes_planes[:, 3, :])
+        ms_raw.append(load("ms_raw1", [P, PACK, BANK], F32, mstore_planes[:, :, BANK:M]))
+        notes_raw.extend(load("notes_raw%d" % t, [P, U], F32, notes_planes[:, t, :]) for t in range(1, PACK))
         q2_raw = load("q2_raw", [P, PACK, Q], F32, query2.rearrange(by_plane, t=PACK))
+        memory_list = load("memory_list", [P, Q // PER_COLUMN], U16, offs3)
+        vals_raw = [load("vals_raw%d" % t, [P, T], F32, vals_planes[:, t, :]) for t in range(PACK)]
         with nc.allow_non_contiguous_dma(reason="one factor to a partition"):
-            lam_col = [load("lam%d" % h, [P, 1], F32, lam[h * P : (h + 1) * P, :], queue=nc.sync) for h in range(2)]
-        factor = load("factor", [P, PACK], F32, slot_factor.rearrange("o (s r) -> (o s) r", r=PACK), queue=nc.sync)
-        vals_raw[0] = load("vals_raw0", [P, T], F32, vals_planes[:, 0, :])
-        vals_raw[1] = load("vals_raw1", [P, T], F32, vals_planes[:, 1, :])
-        vals_raw[2] = load("vals_raw2", [P, T], F32, vals_planes[:, 2, :], tag="v2")
-        vals_raw[3] = load("vals_raw3", [P, T], F32, vals_planes[:, 3, :], tag="v3")
-
-        def wide_bank(name, tag):
-            return ps.tile([P, BANK], F32, name=name, tag=tag, bufs=4)
+            lam_col = [load("lam%d" % h, [P, 1], F32, lam[h * P : (h + 1) * P, :], nc.gpsimd) for h in range(Q // P)]
+        factor = load("factor", [P, PACK], F32, slot_factor.rearrange("o (s r) -> (o s) r", r=PACK), nc.gpsimd)
 
         memory = [tile("memory%d" % t, [P, M], F32) for t in range(PACK)]
         notes_picked = tile("notes_picked", [P, PACK, I], BF16)
         weights = tile("weights", [P, Q * PACK], BF16)
         dealt = "p (s r) -> p r s"
-        out_planes = out_0.rearrange(by_plane, t=PACK)
 
-        def memories(half, ms_q):
+        def memories(half):
+            ms_q = quantise("ms%d" % half, weave(nc.vector, "ms_woven%d" % half, ms_raw[half][:], BANK))
             for t in range(PACK):
-                bank = wide_bank("me_ps", "other")
-                product(bank[:], wm_q, slice(t * P, (t + 1) * P), ms_q, FP8X4)
-                nc.scalar.copy(out=memory[t][:, half * BANK : (half + 1) * BANK], in_=bank[:])
+                me = bank("me")
+                product(me[:], wm_q, t, ms_q)
+                nc.scalar.copy(out=memory[t][:, half * BANK : (half + 1) * BANK], in_=me[:])
+
+        def pick_notes(engine, t):
+            gather(engine, notes_picked[:, t, :], notes_raw[t], note_list[:])
 
         def token_scores(h):
-            a = wide_bank("a_ps", "score")
-            product(a[:], q_q, slice(h * P, (h + 1) * P), keys, FP4X4)
+            a = bank("a")
+            product(a[:], q_q, h, keys, FP4X4)
             a_sb = tile("a_sb%d" % h, [P, PACK, P], F32)
             nc.scalar.copy(out=a_sb[:], in_=a[:].rearrange(dealt, r=PACK))
             return a_sb
 
-        def scores(h):
-            b = wide_bank("b_ps", "score")
-            product(b[:], q2_q, slice(h * P, (h + 1) * P), notes_q, FP8X4)
+        def note_scores(h):
+            b = bank("b")
+            product(b[:], q2_q, h, notes_q)
+            return b
+
+        def weigh(h):
+            b = b_ps[h][:].rearrange(dealt, r=PACK)
             larger = tile("larger%d" % h, [P, PACK, P], F32)
             smaller = tile("smaller%d" % h, [P, PACK, P], F32)
-            nc.vector.tensor_tensor(out=larger[:], in0=b[:].rearrange(dealt, r=PACK), in1=a_sb[h][:], op=ALU.max)
-            nc.vector.tensor_tensor(out=smaller[:], in0=b[:].rearrange(dealt, r=PACK), in1=a_sb[h][:], op=ALU.min)
+            nc.vector.tensor_tensor(out=larger[:], in0=b, in1=a_sb[h][:], op=ALU.max)
+            nc.vector.tensor_tensor(out=smaller[:], in0=b, in1=a_sb[h][:], op=ALU.min)
             score = tile("score%d" % h, [P, PACK, P], F32)
             nc.vector.scalar_tensor_tensor(
                 out=score[:], in0=smaller[:], scalar=lam_col[h][:], in1=larger[:], op0=ALU.mult, op1=ALU.add
             )
-            turned = wide_bank("turned_ps", "score")
+            turned = bank("turned")
             for r in range(PACK):
                 nc.tensor.transpose(turned[:, r * P : (r + 1) * P], score[:, r, :], identity[:])
             nc.vector.scalar_tensor_tensor(
@@ -158,70 +165,86 @@ def tile_attend_twopools_remembered_lean_pl_kernel(
                 op1=ALU.mult,
             )
 
-        def pick_values(t, engine):
-            picked = tile("vals_picked%d" % t, [P, I], BF16)
-            if engine is None:
-                gather_shared(picked, vals_raw[t], token_list, I)
-            else:
-                gather(engine, picked[:], vals_raw[t], token_list[:])
-            return picked
+        def turn_values(picked):
+            pairs = picked[:].bitcast(F32)
+            turned = bank("pairs")[:, 0 : 2 * P].rearrange("p (u e) -> p u e", u=2)
+            for u in range(2):
+                nc.tensor.transpose(turned[:, u, :], pairs[:, u : I // 2 : 2], identity[:])
+            return turned
 
-        def turn_values(t0, picked, engine, bank, words):
-            n = len(picked)
-            pairs_ps = bank[:, 0 : n * 2 * P].rearrange("p (k u e) -> p k u e", k=n, u=2)
+        def lay_values(turned, words):
+            nc.scalar.copy(out=words.rearrange("p (e u) -> p e u", u=2), in_=turned.rearrange("p u e -> p e u"))
+
+        def weighted_values(n, v_q):
+            o = bank("o")[:, 0 : n * Q].rearrange("p (k q) -> p k q", k=n)
             for k in range(n):
-                pairs = picked[k][:].bitcast(F32)
-                for u in range(2):
-                    nc.tensor.transpose(pairs_ps[:, k, u, :], pairs[:, u : I // 2 : 2], identity[:])
-            copy(
-                engine,
-                words.rearrange("p (k e u) -> p k e u", k=n, u=2),
-                pairs_ps.rearrange("p k u e -> p k e u"),
-            )
-            return quantise("v%d" % t0, words.bitcast(BF16), n * P)
+                product(o[:, k, :], v_q, k, w_q)
+            return o
 
-        def result(t0, n, v_q, bank):
-            o = bank[:, 0 : n * Q].rearrange("p (k q) -> p k q", k=n)
-            for k in range(n):
-                product(o[:, k, :], v_q, slice(k * P, (k + 1) * P), w_q, FP8X4)
-            nc.vector.tensor_tensor(out=y[:, t0 : t0 + n, :], in0=o, in1=recalled[:, t0 : t0 + n, :], op=ALU.mult)
-            nc.sync.dma_start(out=out_planes[:, t0 : t0 + n, :], in_=y[:, t0 : t0 + n, :])
+        def result(t0, o):
+            planes = slice(t0, t0 + o.shape[1])
+            nc.vector.tensor_tensor(out=y[:, planes, :], in0=o, in1=recalled[:, planes, :], op=ALU.mult)
+            nc.sync.dma_start(out=out_planes[:, planes, :], in_=y[:, planes, :])
 
+        keys = tile("keys", [P, I], U16)[:], tile("keys_sc", [P, I], U8)[:]
+        gather(nc.vector, keys[0], key_words, token_list[:])
+        gather(nc.vector, keys[1], key_scales, token_list[:])
         wm_woven = tile("wm_woven", [P, E * PACK], BF16)
-        copy(nc.vector, wm_woven[:].rearrange("p (t m j) -> p m j t", t=PACK, j=PACK), wm_raw[:].rearrange("p j (m t) -> p m j t", t=PACK))
-        wm_q = quantise("wm", wm_woven[:], E)
-        memories(0, quantise("ms0", weave(nc.vector, "ms_woven0", ms_raw[0][:], BANK)[:], BANK))
-        gather(nc.scalar, notes_picked[:, 0, :], notes_raw[0], note_list[:])
-        keys = tile("keys", [P, I], U16), tile("keys_sc", [P, I], U8)
-        gather(nc.vector, keys[0][:], key_words, token_list[:])
-        gather(nc.vector, keys[1][:], key_scales, token_list[:])
-        memories(1, quantise("ms1", weave(nc.vector, "ms_woven1", ms_raw[1][:], BANK)[:], BANK))
-        gather(nc.scalar, notes_picked[:, 1, :], notes_raw[1], note_list[:])
-        q_q = quantise("q", weave(nc.vector, "q_woven", q_raw[:], Q)[:], Q)
-        a_sb = [token_scores(h) for h in range(2)]
-        gather(nc.vector, notes_picked[:, 2, :], notes_raw[2], note_list[:])
-        gather(nc.vector, notes_picked[:, 3, :], notes_raw[3], note_list[:])
-        notes_q = quantise("notes", weave(nc.vector, "notes_woven", notes_picked[:], I)[:], I)
-        q2_q = quantise("q2", weave(nc.vector, "q2_woven", q2_raw[:], Q)[:], Q)
-        recalled = tile("recalled", [P, PACK, Q], F32, "")
+        nc.vector.tensor_copy(
+            out=wm_woven[:].rearrange("p (t m j) -> p m j t", t=PACK, j=PACK),
+            in_=wm_raw[:].rearrange("p j (m t) -> p m j t", t=PACK),
+        )
+        wm_q = quantise("wm", wm_woven[:])
+        memories(0)
+        pick_notes(nc.scalar, 0)
+        q_q = quantise("q", weave(nc.vector, "q_woven", q_raw[:], Q))
+        a_sb = [token_scores(h) for h in range(Q // P)]
+        memories(1)
+        pick_notes(nc.scalar, 1)
+        pick_notes(nc.vector, 2)
+        pick_notes(nc.vector, 3)
+        notes_q = quantise("notes", weave(nc.vector, "notes_woven", notes_picked[:], I))
+        q2_q = quantise("q2", weave(nc.scalar, "q2_woven", q2_raw[:], Q))
+        recalled = tile("recalled", [P, PACK, Q], F32)
         for t in range(PACK):
             gather(nc.scalar, recalled[:, t, :], memory[t], memory_list[:])
-        scores(0)
-        scores(1)
-        w_q = quantise("w", weights[:], Q)
-        y_flat = tile("y", [P, PACK * Q], F32)
-        y = y_flat[:].rearrange("p (t q) -> p t q", t=PACK)
-        picked = [pick_values(t, nc.scalar) for t in range(PACK)]
-        v0 = turn_values(0, picked[0:1], nc.scalar, wide_bank("pairs_ps", "other"), tile("v_words0", [P, 2 * P], F32, "v2")[:])
-        v12 = turn_values(1, picked[1:3], nc.scalar, wide_bank("pairs_ps", "other"), tile("v_words12", [P, 4 * P], F32, "v3")[:])
-        last_bank = wide_bank("last_ps", "other")
-        v3 = turn_values(3, picked[3:4], nc.scalar, last_bank, y_flat[:, P : 3 * P])
-        result(0, 1, v0, wide_bank("o_ps", "other"))
-        result(1, 2, v12, last_bank)
-        result(3, 1, v3, wide_bank("o_ps", "other"))
+        b_ps = [note_scores(h) for h in range(Q // P)]
 
-        y_codes, y_scales = quantise("y", weave(nc.vector, "y_woven", y[:], Q)[:], Q)
-        nc.sync.dma_start(out=out_1[0].rearrange("p n t -> p (n t)").bitcast(I32), in_=y_codes[:].bitcast(I32))
+        picked = [tile("vals_picked%d" % t, [P, I], BF16) for t in range(2)]
+        turned = []
+        for t in range(2):
+            gather(nc.scalar, picked[t][:], vals_raw[t], token_list[:])
+            turned.append(turn_values(picked[t]))
+            weigh(t)
+        picked.append(late_tile("vals_picked2", [P, I], BF16))
+        gather(nc.scalar, picked[2][:], vals_raw[2], token_list[:])
+        turned.append(turn_values(picked[2]))
+        words01 = late_tile("words01", [P, 2 * Q], F32)
+        for t in range(2):
+            lay_values(turned[t], words01[:, t * Q : (t + 1) * Q])
+        v01 = quantise("v01", words01[:].bitcast(BF16), "codes", 2)
+        w_q = quantise("w", weights[:], "codes", 2)
+        words2 = late_tile("words2", [P, Q], F32)
+        lay_values(turned[2], words2[:])
+        picked.append(late_tile("vals_picked3", [P, I], BF16))
+        gather(nc.scalar, picked[3][:, 0:LAST_SHARE], vals_raw[3], token_list[:, 0 : LAST_SHARE // PER_COLUMN])
+        gather(nc.vector, picked[3][:, LAST_SHARE:I], vals_raw[3], token_list[:, LAST_SHARE // PER_COLUMN : I // PER_COLUMN])
+        v2 = quantise("v2", words2[:].bitcast(BF16), "late", 6)
+        o01 = weighted_values(2, v01)
+        turned.append(turn_values(picked[3]))
+        y_flat = late_tile("y", [P, PACK * Q], F32)
+        y = y_flat[:].rearrange("p (t q) -> p t q", t=PACK)
+        result(0, o01)
+        y_woven = tile("y_woven", [P, Q, PACK], BF16)
+        nc.scalar.copy(out=y_woven[:, :, 0:2], in_=y[:, 0:2, :].rearrange("p t q -> p q t"))
+        lay_values(turned[3], y_flat[:, 2 * Q : 3 * Q])
+        v3 = quantise("v3", y_flat[:, 2 * Q : 3 * Q].bitcast(BF16))
+        result(2, weighted_values(1, v2))
+        result(3, weighted_values(1, v3))
+        nc.vector.tensor_copy(out=y_woven[:, :, 2:4], in_=y[:, 2:4, :].rearrange("p t q -> p q t"))
+
+        y_codes, y_scales = quantise("y", y_woven[:].rearrange("p q t -> p (q t)"))
+        nc.sync.dma_start(out=out_1[0].rearrange("p n t -> p (n t)").bitcast(I32), in_=y_codes.bitcast(I32))
         for quad in range(4):
             queue = nc.sync if quad < 2 else nc.scalar
             queue.dma_start(

@@ -22,7 +22,7 @@ PACK = 4
 BANK = 512
 BANKS = 8
 PER_COLUMN = 16
-LAST_SHARE = 352
+LAST_SHARE = 288
 
 
 def tile_attend_twopools_remembered_lean_pl_kernel(
@@ -38,7 +38,7 @@ def tile_attend_twopools_remembered_lean_pl_kernel(
             return sb.tile(shape, dtype, name=name, tag=tag, bufs=bufs, align_bytes=64)
 
         def late_tile(name, shape, dtype):
-            return tile(name, shape, dtype, "late", 6)
+            return tile(name, shape, dtype, "late", 10)
 
         def bank(name):
             return ps.tile([P, BANK], F32, name=name, tag="bank", bufs=BANKS)
@@ -85,6 +85,9 @@ def tile_attend_twopools_remembered_lean_pl_kernel(
 
         key_scales = tile("key_scales", [P, T], U8)
         nc.vector.memset(key_scales[:].bitcast(U32), 0)
+        with nc.allow_non_contiguous_dma(reason="one factor to a partition"):
+            lam_col = [load("lam%d" % h, [P, 1], F32, lam[h * P : (h + 1) * P, :], nc.gpsimd) for h in range(Q // P)]
+        factor = load("factor", [P, PACK], F32, slot_factor.rearrange("o (s r) -> (o s) r", r=PACK), nc.gpsimd)
         identity = tile("identity", [P, P], F32)
         make_identity(nc, identity[:])
 
@@ -103,8 +106,8 @@ def tile_attend_twopools_remembered_lean_pl_kernel(
                 in_=keys_scales[0][4 * quad : 4 * quad + 4, :].bitcast(I32),
             )
         wm_raw = load("wm_raw", [P, PACK, E], F32, wm.rearrange(by_plane, t=PACK))
-        note_list = load("note_list", [P, I // PER_COLUMN], U16, offs2)
         ms_raw = [load("ms_raw0", [P, PACK, BANK], F32, mstore_planes[:, :, 0:BANK])]
+        note_list = load("note_list", [P, I // PER_COLUMN], U16, offs2)
         notes_raw = [load("notes_raw0", [P, U], F32, notes_planes[:, 0, :])]
         q_raw = load("q_raw", [P, PACK, Q], F32, query.rearrange(by_plane, t=PACK))
         ms_raw.append(load("ms_raw1", [P, PACK, BANK], F32, mstore_planes[:, :, BANK:M]))
@@ -112,14 +115,10 @@ def tile_attend_twopools_remembered_lean_pl_kernel(
         q2_raw = load("q2_raw", [P, PACK, Q], F32, query2.rearrange(by_plane, t=PACK))
         memory_list = load("memory_list", [P, Q // PER_COLUMN], U16, offs3)
         vals_raw = [load("vals_raw%d" % t, [P, T], F32, vals_planes[:, t, :]) for t in range(PACK)]
-        with nc.allow_non_contiguous_dma(reason="one factor to a partition"):
-            lam_col = [load("lam%d" % h, [P, 1], F32, lam[h * P : (h + 1) * P, :], nc.gpsimd) for h in range(Q // P)]
-        factor = load("factor", [P, PACK], F32, slot_factor.rearrange("o (s r) -> (o s) r", r=PACK), nc.gpsimd)
 
         memory = [tile("memory%d" % t, [P, M], F32) for t in range(PACK)]
         notes_picked = tile("notes_picked", [P, PACK, I], BF16)
         weights = tile("weights", [P, Q * PACK], BF16)
-        dealt = "p (s r) -> p r s"
 
         def memories(half):
             ms_q = quantise("ms%d" % half, weave(nc.vector, "ms_woven%d" % half, ms_raw[half][:], BANK))
@@ -135,7 +134,7 @@ def tile_attend_twopools_remembered_lean_pl_kernel(
             a = bank("a")
             product(a[:], q_q, h, keys, FP4X4)
             a_sb = tile("a_sb%d" % h, [P, PACK, P], F32)
-            nc.scalar.copy(out=a_sb[:], in_=a[:].rearrange(dealt, r=PACK))
+            nc.scalar.copy(out=a_sb[:].rearrange("p r s -> p s r"), in_=a[:].rearrange("p (s r) -> p s r", r=PACK))
             return a_sb
 
         def note_scores(h):
@@ -144,7 +143,7 @@ def tile_attend_twopools_remembered_lean_pl_kernel(
             return b
 
         def weigh(h):
-            b = b_ps[h][:].rearrange(dealt, r=PACK)
+            b = b_ps[h][:].rearrange("p (r s) -> p r s", r=PACK)
             larger = tile("larger%d" % h, [P, PACK, P], F32)
             smaller = tile("smaller%d" % h, [P, PACK, P], F32)
             nc.vector.tensor_tensor(out=larger[:], in0=b, in1=a_sb[h][:], op=ALU.max)
@@ -181,10 +180,10 @@ def tile_attend_twopools_remembered_lean_pl_kernel(
                 product(o[:, k, :], v_q, k, w_q)
             return o
 
-        def result(t0, o):
+        def result(t0, o, y):
             planes = slice(t0, t0 + o.shape[1])
-            nc.vector.tensor_tensor(out=y[:, planes, :], in0=o, in1=recalled[:, planes, :], op=ALU.mult)
-            nc.sync.dma_start(out=out_planes[:, planes, :], in_=y[:, planes, :])
+            nc.vector.tensor_tensor(out=y, in0=o, in1=recalled[:, planes, :], op=ALU.mult)
+            nc.sync.dma_start(out=out_planes[:, planes, :], in_=y)
 
         keys = tile("keys", [P, I], U16)[:], tile("keys_sc", [P, I], U8)[:]
         gather(nc.vector, keys[0], key_words, token_list[:])
@@ -203,8 +202,13 @@ def tile_attend_twopools_remembered_lean_pl_kernel(
         pick_notes(nc.scalar, 1)
         pick_notes(nc.vector, 2)
         pick_notes(nc.vector, 3)
-        notes_q = quantise("notes", weave(nc.vector, "notes_woven", notes_picked[:], I))
-        q2_q = quantise("q2", weave(nc.scalar, "q2_woven", q2_raw[:], Q))
+        notes_woven = tile("notes_woven", [P, I * PACK], BF16)
+        nc.vector.tensor_copy(
+            out=notes_woven[:].rearrange("p (r s t) -> p s t r", r=PACK, t=PACK),
+            in_=notes_picked[:].rearrange("p t (s r) -> p s t r", r=PACK),
+        )
+        notes_q = quantise("notes", notes_woven[:])
+        q2_q = quantise("q2", weave(nc.vector, "q2_woven", q2_raw[:], Q))
         recalled = tile("recalled", [P, PACK, Q], F32)
         for t in range(PACK):
             gather(nc.scalar, recalled[:, t, :], memory[t], memory_list[:])
@@ -229,19 +233,20 @@ def tile_attend_twopools_remembered_lean_pl_kernel(
         picked.append(late_tile("vals_picked3", [P, I], BF16))
         gather(nc.scalar, picked[3][:, 0:LAST_SHARE], vals_raw[3], token_list[:, 0 : LAST_SHARE // PER_COLUMN])
         gather(nc.vector, picked[3][:, LAST_SHARE:I], vals_raw[3], token_list[:, LAST_SHARE // PER_COLUMN : I // PER_COLUMN])
-        v2 = quantise("v2", words2[:].bitcast(BF16), "late", 6)
+        v2 = quantise("v2", words2[:].bitcast(BF16), "late", 10)
         o01 = weighted_values(2, v01)
         turned.append(turn_values(picked[3]))
-        y_flat = late_tile("y", [P, PACK * Q], F32)
-        y = y_flat[:].rearrange("p (t q) -> p t q", t=PACK)
-        result(0, o01)
-        y_woven = tile("y_woven", [P, Q, PACK], BF16)
-        nc.scalar.copy(out=y_woven[:, :, 0:2], in_=y[:, 0:2, :].rearrange("p t q -> p q t"))
-        lay_values(turned[3], y_flat[:, 2 * Q : 3 * Q])
-        v3 = quantise("v3", y_flat[:, 2 * Q : 3 * Q].bitcast(BF16))
-        result(2, weighted_values(1, v2))
-        result(3, weighted_values(1, v3))
-        nc.vector.tensor_copy(out=y_woven[:, :, 2:4], in_=y[:, 2:4, :].rearrange("p t q -> p q t"))
+        y01 = late_tile("y01", [P, 2, Q], F32)
+        result(0, o01, y01[:])
+        words3 = late_tile("words3", [P, Q], F32)
+        lay_values(turned[3], words3[:])
+        y_woven = late_tile("y_woven", [P, Q, PACK], BF16)
+        nc.scalar.copy(out=y_woven[:, :, 0:2], in_=y01[:].rearrange("p t q -> p q t"))
+        v3 = quantise("v3", words3[:].bitcast(BF16), "late", 10)
+        y23 = late_tile("y23", [P, 2, Q], F32)
+        result(2, weighted_values(1, v2), y23[:, 0:1, :])
+        result(3, weighted_values(1, v3), y23[:, 1:2, :])
+        nc.vector.tensor_copy(out=y_woven[:, :, 2:4], in_=y23[:].rearrange("p t q -> p q t"))
 
         y_codes, y_scales = quantise("y", y_woven[:].rearrange("p q t -> p (q t)"))
         nc.sync.dma_start(out=out_1[0].rearrange("p n t -> p (n t)").bitcast(I32), in_=y_codes.bitcast(I32))

@@ -19,10 +19,14 @@ COPY = mybir.ActivationFunctionType.Copy
 
 P = 128
 PACK = 4
+QUADRANT = 32
+SCALE_ROWS = 16
 BANK = 512
 BANKS = 8
 PER_COLUMN = 16
-LAST_SHARE = 288
+RUN = 4
+LAST_SHARE = I // 2
+LATE_TILES = 10
 
 
 def tile_attend_twopools_remembered_lean_pl_kernel(
@@ -38,21 +42,15 @@ def tile_attend_twopools_remembered_lean_pl_kernel(
             return sb.tile(shape, dtype, name=name, tag=tag, bufs=bufs, align_bytes=64)
 
         def late_tile(name, shape, dtype):
-            return tile(name, shape, dtype, "late", 10)
+            return tile(name, shape, dtype, "late", LATE_TILES)
 
         def bank(name):
             return ps.tile([P, BANK], F32, name=name, tag="bank", bufs=BANKS)
 
-        def load(name, shape, dtype, src, queue=nc.sync):
-            t = tile(name, shape, dtype)
-            queue.dma_start(out=t[:], in_=src)
-            return t
-
-        def copy(engine, out, in_):
-            if engine is nc.vector:
-                nc.vector.tensor_copy(out=out, in_=in_)
-            else:
-                nc.scalar.copy(out=out, in_=in_)
+        def load(name, shape, dtype, src):
+            loaded = tile(name, shape, dtype)
+            nc.sync.dma_start(out=loaded[:], in_=src)
+            return loaded
 
         def gather(engine, out, window, offsets):
             if engine is nc.vector:
@@ -60,12 +58,19 @@ def tile_attend_twopools_remembered_lean_pl_kernel(
             else:
                 nc.scalar.activation(out=out, in_=window[:].indirect(offsets), func=COPY)
 
-        def weave(engine, name, planes, width):
+        def weave(name, planes, width):
             woven = tile(name, [P, width * PACK], BF16)
-            copy(
-                engine,
-                woven[:].rearrange("p (c i t) -> p c t i", i=4, t=PACK),
-                planes.rearrange("p t (c i) -> p c t i", i=4),
+            nc.vector.tensor_copy(
+                out=woven[:].rearrange("p (c i t) -> p c t i", i=RUN, t=PACK),
+                in_=planes.rearrange("p t (c i) -> p c t i", i=RUN),
+            )
+            return woven[:]
+
+        def weave_dealt(name, planes, width):
+            woven = tile(name, [P, width * PACK], BF16)
+            nc.vector.tensor_copy(
+                out=woven[:].rearrange("p (r s t) -> p s t r", r=PACK, t=PACK),
+                in_=planes.rearrange("p t (s r) -> p s t r", r=PACK),
             )
             return woven[:]
 
@@ -85,9 +90,6 @@ def tile_attend_twopools_remembered_lean_pl_kernel(
 
         key_scales = tile("key_scales", [P, T], U8)
         nc.vector.memset(key_scales[:].bitcast(U32), 0)
-        with nc.allow_non_contiguous_dma(reason="one factor to a partition"):
-            lam_col = [load("lam%d" % h, [P, 1], F32, lam[h * P : (h + 1) * P, :], nc.gpsimd) for h in range(Q // P)]
-        factor = load("factor", [P, PACK], F32, slot_factor.rearrange("o (s r) -> (o s) r", r=PACK), nc.gpsimd)
         identity = tile("identity", [P, P], F32)
         make_identity(nc, identity[:])
 
@@ -97,23 +99,27 @@ def tile_attend_twopools_remembered_lean_pl_kernel(
         mstore_planes = mstore.rearrange(by_plane, t=PACK)
         out_planes = out_0.rearrange(by_plane, t=PACK)
 
-        key_words = tile("key_words", [P, T], U16)
-        nc.sync.dma_start(out=key_words[:].bitcast(I32), in_=keys_words[0].bitcast(I32))
-        token_list = load("token_list", [P, I // PER_COLUMN], U16, offs)
-        for quad in range(4):
-            nc.sync.dma_start(
-                out=key_scales[32 * quad : 32 * quad + 4, :].bitcast(I32),
-                in_=keys_scales[0][4 * quad : 4 * quad + 4, :].bitcast(I32),
-            )
         wm_raw = load("wm_raw", [P, PACK, E], F32, wm.rearrange(by_plane, t=PACK))
+        for r in range(PACK):
+            nc.sync.dma_start(
+                out=key_scales[r:P:QUADRANT, :].bitcast(I32),
+                in_=keys_scales[0][r:SCALE_ROWS:PACK, :].bitcast(I32),
+            )
         ms_raw = [load("ms_raw0", [P, PACK, BANK], F32, mstore_planes[:, :, 0:BANK])]
         note_list = load("note_list", [P, I // PER_COLUMN], U16, offs2)
         notes_raw = [load("notes_raw0", [P, U], F32, notes_planes[:, 0, :])]
-        q_raw = load("q_raw", [P, PACK, Q], F32, query.rearrange(by_plane, t=PACK))
+        key_words = tile("key_words", [P, T], U16)
+        nc.sync.dma_start(out=key_words[:].bitcast(I32), in_=keys_words[0].bitcast(I32))
+        token_list = load("token_list", [P, I // PER_COLUMN], U16, offs)
         ms_raw.append(load("ms_raw1", [P, PACK, BANK], F32, mstore_planes[:, :, BANK:M]))
-        notes_raw.extend(load("notes_raw%d" % t, [P, U], F32, notes_planes[:, t, :]) for t in range(1, PACK))
-        q2_raw = load("q2_raw", [P, PACK, Q], F32, query2.rearrange(by_plane, t=PACK))
+        notes_raw.append(load("notes_raw1", [P, U], F32, notes_planes[:, 1, :]))
+        q_raw = load("q_raw", [P, PACK, Q], F32, query.rearrange(by_plane, t=PACK))
         memory_list = load("memory_list", [P, Q // PER_COLUMN], U16, offs3)
+        notes_raw.extend(load("notes_raw%d" % t, [P, U], F32, notes_planes[:, t, :]) for t in range(2, PACK))
+        q2_raw = load("q2_raw", [P, PACK, Q], F32, query2.rearrange(by_plane, t=PACK))
+        with nc.allow_non_contiguous_dma(reason="one factor to a partition"):
+            lam_col = [load("lam%d" % h, [P, 1], F32, lam[h * P : (h + 1) * P, :]) for h in range(Q // P)]
+        factor = load("factor", [P, PACK], F32, slot_factor.rearrange("o (s r) -> (o s) r", r=PACK))
         vals_raw = [load("vals_raw%d" % t, [P, T], F32, vals_planes[:, t, :]) for t in range(PACK)]
 
         memory = [tile("memory%d" % t, [P, M], F32) for t in range(PACK)]
@@ -121,7 +127,7 @@ def tile_attend_twopools_remembered_lean_pl_kernel(
         weights = tile("weights", [P, Q * PACK], BF16)
 
         def memories(half):
-            ms_q = quantise("ms%d" % half, weave(nc.vector, "ms_woven%d" % half, ms_raw[half][:], BANK))
+            ms_q = quantise("ms%d" % half, weave("ms_woven%d" % half, ms_raw[half][:], BANK))
             for t in range(PACK):
                 me = bank("me")
                 product(me[:], wm_q, t, ms_q)
@@ -133,9 +139,9 @@ def tile_attend_twopools_remembered_lean_pl_kernel(
         def token_scores(h):
             a = bank("a")
             product(a[:], q_q, h, keys, FP4X4)
-            a_sb = tile("a_sb%d" % h, [P, PACK, P], F32)
-            nc.scalar.copy(out=a_sb[:].rearrange("p r s -> p s r"), in_=a[:].rearrange("p (s r) -> p s r", r=PACK))
-            return a_sb
+            dealt = tile("a_sb%d" % h, [P, PACK, P], F32)
+            nc.scalar.copy(out=dealt[:].rearrange("p r s -> p s r"), in_=a[:].rearrange("p (s r) -> p s r", r=PACK))
+            return dealt
 
         def note_scores(h):
             b = bank("b")
@@ -152,27 +158,29 @@ def tile_attend_twopools_remembered_lean_pl_kernel(
             nc.vector.scalar_tensor_tensor(
                 out=score[:], in0=smaller[:], scalar=lam_col[h][:], in1=larger[:], op0=ALU.mult, op1=ALU.add
             )
-            turned = bank("turned")
+            score_turned = bank("score_turned")
             for r in range(PACK):
-                nc.tensor.transpose(turned[:, r * P : (r + 1) * P], score[:, r, :], identity[:])
+                nc.tensor.transpose(score_turned[:, r * P : (r + 1) * P], score[:, r, :], identity[:])
             nc.vector.scalar_tensor_tensor(
                 out=weights[:, h * BANK : (h + 1) * BANK].rearrange("p (q r) -> p q r", r=PACK),
-                in0=turned[:].rearrange("p (r q) -> p q r", r=PACK),
+                in0=score_turned[:].rearrange("p (r q) -> p q r", r=PACK),
                 scalar=0.0,
                 in1=factor[:].unsqueeze(1).to_broadcast([P, P, PACK]),
                 op0=ALU.max,
                 op1=ALU.mult,
             )
 
-        def turn_values(picked):
-            pairs = picked[:].bitcast(F32)
-            turned = bank("pairs")[:, 0 : 2 * P].rearrange("p (u e) -> p u e", u=2)
+        def turn_values(plane):
+            pairs = plane[:].bitcast(F32)
+            pairs_turned = bank("pairs_turned")[:, 0 : 2 * P].rearrange("p (u e) -> p u e", u=2)
             for u in range(2):
-                nc.tensor.transpose(turned[:, u, :], pairs[:, u : I // 2 : 2], identity[:])
-            return turned
+                nc.tensor.transpose(pairs_turned[:, u, :], pairs[:, u : I // 2 : 2], identity[:])
+            return pairs_turned
 
-        def lay_values(turned, words):
-            nc.scalar.copy(out=words.rearrange("p (e u) -> p e u", u=2), in_=turned.rearrange("p u e -> p e u"))
+        def lay_values(pairs_turned, words):
+            nc.scalar.copy(
+                out=words.rearrange("p (e u) -> p e u", u=2), in_=pairs_turned.rearrange("p u e -> p e u")
+            )
 
         def weighted_values(n, v_q):
             o = bank("o")[:, 0 : n * Q].rearrange("p (k q) -> p k q", k=n)
@@ -185,30 +193,20 @@ def tile_attend_twopools_remembered_lean_pl_kernel(
             nc.vector.tensor_tensor(out=y, in0=o, in1=recalled[:, planes, :], op=ALU.mult)
             nc.sync.dma_start(out=out_planes[:, planes, :], in_=y)
 
+        wm_q = quantise("wm", weave_dealt("wm_woven", wm_raw[:], E))
+        memories(0)
+        pick_notes(nc.scalar, 0)
         keys = tile("keys", [P, I], U16)[:], tile("keys_sc", [P, I], U8)[:]
         gather(nc.vector, keys[0], key_words, token_list[:])
         gather(nc.vector, keys[1], key_scales, token_list[:])
-        wm_woven = tile("wm_woven", [P, E * PACK], BF16)
-        nc.vector.tensor_copy(
-            out=wm_woven[:].rearrange("p (t m j) -> p m j t", t=PACK, j=PACK),
-            in_=wm_raw[:].rearrange("p j (m t) -> p m j t", t=PACK),
-        )
-        wm_q = quantise("wm", wm_woven[:])
-        memories(0)
-        pick_notes(nc.scalar, 0)
-        q_q = quantise("q", weave(nc.vector, "q_woven", q_raw[:], Q))
-        a_sb = [token_scores(h) for h in range(Q // P)]
         memories(1)
         pick_notes(nc.scalar, 1)
+        q_q = quantise("q", weave("q_woven", q_raw[:], Q))
+        a_sb = [token_scores(h) for h in range(Q // P)]
         pick_notes(nc.vector, 2)
         pick_notes(nc.vector, 3)
-        notes_woven = tile("notes_woven", [P, I * PACK], BF16)
-        nc.vector.tensor_copy(
-            out=notes_woven[:].rearrange("p (r s t) -> p s t r", r=PACK, t=PACK),
-            in_=notes_picked[:].rearrange("p t (s r) -> p s t r", r=PACK),
-        )
-        notes_q = quantise("notes", notes_woven[:])
-        q2_q = quantise("q2", weave(nc.vector, "q2_woven", q2_raw[:], Q))
+        notes_q = quantise("notes", weave_dealt("notes_woven", notes_picked[:], I))
+        q2_q = quantise("q2", weave("q2_woven", q2_raw[:], Q))
         recalled = tile("recalled", [P, PACK, Q], F32)
         for t in range(PACK):
             gather(nc.scalar, recalled[:, t, :], memory[t], memory_list[:])
@@ -230,10 +228,12 @@ def tile_attend_twopools_remembered_lean_pl_kernel(
         w_q = quantise("w", weights[:], "codes", 2)
         words2 = late_tile("words2", [P, Q], F32)
         lay_values(turned[2], words2[:])
+
         picked.append(late_tile("vals_picked3", [P, I], BF16))
-        gather(nc.scalar, picked[3][:, 0:LAST_SHARE], vals_raw[3], token_list[:, 0 : LAST_SHARE // PER_COLUMN])
-        gather(nc.vector, picked[3][:, LAST_SHARE:I], vals_raw[3], token_list[:, LAST_SHARE // PER_COLUMN : I // PER_COLUMN])
-        v2 = quantise("v2", words2[:].bitcast(BF16), "late", 10)
+        cut = LAST_SHARE // PER_COLUMN
+        gather(nc.scalar, picked[3][:, 0:LAST_SHARE], vals_raw[3], token_list[:, 0:cut])
+        gather(nc.vector, picked[3][:, LAST_SHARE:I], vals_raw[3], token_list[:, cut : I // PER_COLUMN])
+        v2 = quantise("v2", words2[:].bitcast(BF16), "late", LATE_TILES)
         o01 = weighted_values(2, v01)
         turned.append(turn_values(picked[3]))
         y01 = late_tile("y01", [P, 2, Q], F32)
@@ -242,7 +242,7 @@ def tile_attend_twopools_remembered_lean_pl_kernel(
         lay_values(turned[3], words3[:])
         y_woven = late_tile("y_woven", [P, Q, PACK], BF16)
         nc.scalar.copy(out=y_woven[:, :, 0:2], in_=y01[:].rearrange("p t q -> p q t"))
-        v3 = quantise("v3", words3[:].bitcast(BF16), "late", 10)
+        v3 = quantise("v3", words3[:].bitcast(BF16), "late", LATE_TILES)
         y23 = late_tile("y23", [P, 2, Q], F32)
         result(2, weighted_values(1, v2), y23[:, 0:1, :])
         result(3, weighted_values(1, v3), y23[:, 1:2, :])
@@ -250,9 +250,9 @@ def tile_attend_twopools_remembered_lean_pl_kernel(
 
         y_codes, y_scales = quantise("y", y_woven[:].rearrange("p q t -> p (q t)"))
         nc.sync.dma_start(out=out_1[0].rearrange("p n t -> p (n t)").bitcast(I32), in_=y_codes.bitcast(I32))
-        for quad in range(4):
+        for quad in range(P // QUADRANT):
             queue = nc.sync if quad < 2 else nc.scalar
             queue.dma_start(
-                out=out_2[0][4 * quad : 4 * quad + 4, :].bitcast(I32),
-                in_=y_scales[32 * quad : 32 * quad + 4, :].bitcast(I32),
+                out=out_2[0][PACK * quad : PACK * (quad + 1), :].bitcast(I32),
+                in_=y_scales[QUADRANT * quad : QUADRANT * quad + PACK, :].bitcast(I32),
             )

from contextlib import ExitStack

import concourse.mybir as mybir
from concourse.masks import make_identity

D, T, I, Q, E, U, M, C = 512, 2048, 512, 256, 512, 1024, 1024, 512
FLOPS = 2 * (2 * D * Q * I + I * E * Q + C * E * M)

F32 = mybir.dt.float32
BF16 = mybir.dt.bfloat16
I32 = mybir.dt.int32
U32 = mybir.dt.uint32
U16 = mybir.dt.uint16
U8 = mybir.dt.uint8
FP8X4 = mybir.dt.float8_e4m3fn_x4
FP4X4 = mybir.dt.float4_e2m1fn_x4
ALU = mybir.AluOpType
COPY = mybir.ActivationFunctionType.Copy

P = 128
PACK = 4
QUADRANT = 32
SCALE_ROWS = 16
BANK = 512
BANKS = 8
PER_COLUMN = 16
RUN = 4
LAST_SHARE = I // 2
LATE_TILES = 10


def tile_attend_twopools_remembered_lean_pl_kernel(
    tc, query, keys_words, keys_scales, query2, notes, lam, slot_factor, vals, wm, mstore,
    offs, offs2, offs3, out_0, out_1, out_2,
):
    nc = tc.nc
    with ExitStack() as ctx:
        sb = ctx.enter_context(tc.tile_pool(name="sb", bufs=1))
        ps = ctx.enter_context(tc.psum_pool(name="ps", bufs=1))

        def tile(name, shape, dtype, tag="", bufs=None):
            return sb.tile(shape, dtype, name=name, tag=tag, bufs=bufs, align_bytes=64)

        def late_tile(name, shape, dtype):
            return tile(name, shape, dtype, "late", LATE_TILES)

        def bank(name):
            return ps.tile([P, BANK], F32, name=name, tag="bank", bufs=BANKS)

        def load(name, shape, dtype, src):
            loaded = tile(name, shape, dtype)
            nc.sync.dma_start(out=loaded[:], in_=src)
            return loaded

        def gather(engine, out, window, offsets):
            if engine is nc.vector:
                nc.vector.tensor_copy(out=out, in_=window[:].indirect(offsets))
            else:
                nc.scalar.activation(out=out, in_=window[:].indirect(offsets), func=COPY)

        def weave(name, planes, width):
            woven = tile(name, [P, width * PACK], BF16)
            nc.vector.tensor_copy(
                out=woven[:].rearrange("p (c i t) -> p c t i", i=RUN, t=PACK),
                in_=planes.rearrange("p t (c i) -> p c t i", i=RUN),
            )
            return woven[:]

        def weave_dealt(name, planes, width):
            woven = tile(name, [P, width * PACK], BF16)
            nc.vector.tensor_copy(
                out=woven[:].rearrange("p (r s t) -> p s t r", r=PACK, t=PACK),
                in_=planes.rearrange("p t (s r) -> p s t r", r=PACK),
            )
            return woven[:]

        def quantise(name, woven, tag="", bufs=None):
            width = woven.shape[1] // PACK
            codes = tile(name + "_codes", [P, width], U32, tag, bufs)
            scales = tile(name + "_scales", [P, width], U8)
            nc.vector.quantize_mx(out=codes[:].bitcast(FP8X4), scales=scales[:], in_=woven)
            return codes[:], scales[:]

        def product(out, left, block, right, right_dtype=FP8X4):
            cols = slice(block * P, (block + 1) * P)
            nc.tensor.matmul_mx(
                out=out, lhsT=left[0][:, cols].bitcast(FP8X4), lhsT_scale=left[1][:, cols],
                rhs=right[0].bitcast(right_dtype), rhs_scale=right[1], start=True, stop=True,
            )

        key_scales = tile("key_scales", [P, T], U8)
        nc.vector.memset(key_scales[:].bitcast(U32), 0)
        identity = tile("identity", [P, P], F32)
        make_identity(nc, identity[:])

        by_plane = "(p t) n -> p t n"
        notes_planes = notes.rearrange(by_plane, t=PACK)
        vals_planes = vals.rearrange(by_plane, t=PACK)
        mstore_planes = mstore.rearrange(by_plane, t=PACK)
        out_planes = out_0.rearrange(by_plane, t=PACK)

        wm_raw = load("wm_raw", [P, PACK, E], F32, wm.rearrange(by_plane, t=PACK))
        for r in range(PACK):
            nc.sync.dma_start(
                out=key_scales[r:P:QUADRANT, :].bitcast(I32),
                in_=keys_scales[0][r:SCALE_ROWS:PACK, :].bitcast(I32),
            )
        ms_raw = [load("ms_raw0", [P, PACK, BANK], F32, mstore_planes[:, :, 0:BANK])]
        note_list = load("note_list", [P, I // PER_COLUMN], U16, offs2)
        notes_raw = [load("notes_raw0", [P, U], F32, notes_planes[:, 0, :])]
        key_words = tile("key_words", [P, T], U16)
        nc.sync.dma_start(out=key_words[:].bitcast(I32), in_=keys_words[0].bitcast(I32))
        token_list = load("token_list", [P, I // PER_COLUMN], U16, offs)
        ms_raw.append(load("ms_raw1", [P, PACK, BANK], F32, mstore_planes[:, :, BANK:M]))
        notes_raw.append(load("notes_raw1", [P, U], F32, notes_planes[:, 1, :]))
        q_raw = load("q_raw", [P, PACK, Q], F32, query.rearrange(by_plane, t=PACK))
        memory_list = load("memory_list", [P, Q // PER_COLUMN], U16, offs3)
        notes_raw.extend(load("notes_raw%d" % t, [P, U], F32, notes_planes[:, t, :]) for t in range(2, PACK))
        q2_raw = load("q2_raw", [P, PACK, Q], F32, query2.rearrange(by_plane, t=PACK))
        with nc.allow_non_contiguous_dma(reason="one factor to a partition"):
            lam_col = [load("lam%d" % h, [P, 1], F32, lam[h * P : (h + 1) * P, :]) for h in range(Q // P)]
        factor = load("factor", [P, PACK], F32, slot_factor.rearrange("o (s r) -> (o s) r", r=PACK))
        vals_raw = [load("vals_raw%d" % t, [P, T], F32, vals_planes[:, t, :]) for t in range(PACK)]

        memory = [tile("memory%d" % t, [P, M], F32) for t in range(PACK)]
        notes_picked = tile("notes_picked", [P, PACK, I], BF16)
        weights = tile("weights", [P, Q * PACK], BF16)

        def memories(half):
            ms_q = quantise("ms%d" % half, weave("ms_woven%d" % half, ms_raw[half][:], BANK))
            for t in range(PACK):
                me = bank("me")
                product(me[:], wm_q, t, ms_q)
                nc.scalar.copy(out=memory[t][:, half * BANK : (half + 1) * BANK], in_=me[:])

        def pick_notes(engine, t):
            gather(engine, notes_picked[:, t, :], notes_raw[t], note_list[:])

        def token_scores(h):
            a = bank("a")
            product(a[:], q_q, h, keys, FP4X4)
            dealt = tile("a_sb%d" % h, [P, PACK, P], F32)
            nc.scalar.copy(out=dealt[:].rearrange("p r s -> p s r"), in_=a[:].rearrange("p (s r) -> p s r", r=PACK))
            return dealt

        def note_scores(h):
            b = bank("b")
            product(b[:], q2_q, h, notes_q)
            return b

        def weigh(h):
            b = b_ps[h][:].rearrange("p (r s) -> p r s", r=PACK)
            larger = tile("larger%d" % h, [P, PACK, P], F32)
            smaller = tile("smaller%d" % h, [P, PACK, P], F32)
            nc.vector.tensor_tensor(out=larger[:], in0=b, in1=a_sb[h][:], op=ALU.max)
            nc.vector.tensor_tensor(out=smaller[:], in0=b, in1=a_sb[h][:], op=ALU.min)
            score = tile("score%d" % h, [P, PACK, P], F32)
            nc.vector.scalar_tensor_tensor(
                out=score[:], in0=smaller[:], scalar=lam_col[h][:], in1=larger[:], op0=ALU.mult, op1=ALU.add
            )
            score_turned = bank("score_turned")
            for r in range(PACK):
                nc.tensor.transpose(score_turned[:, r * P : (r + 1) * P], score[:, r, :], identity[:])
            nc.vector.scalar_tensor_tensor(
                out=weights[:, h * BANK : (h + 1) * BANK].rearrange("p (q r) -> p q r", r=PACK),
                in0=score_turned[:].rearrange("p (r q) -> p q r", r=PACK),
                scalar=0.0,
                in1=factor[:].unsqueeze(1).to_broadcast([P, P, PACK]),
                op0=ALU.max,
                op1=ALU.mult,
            )

        def turn_values(plane):
            pairs = plane[:].bitcast(F32)
            pairs_turned = bank("pairs_turned")[:, 0 : 2 * P].rearrange("p (u e) -> p u e", u=2)
            for u in range(2):
                nc.tensor.transpose(pairs_turned[:, u, :], pairs[:, u : I // 2 : 2], identity[:])
            return pairs_turned

        def lay_values(pairs_turned, words):
            nc.scalar.copy(
                out=words.rearrange("p (e u) -> p e u", u=2), in_=pairs_turned.rearrange("p u e -> p e u")
            )

        def weighted_values(n, v_q):
            o = bank("o")[:, 0 : n * Q].rearrange("p (k q) -> p k q", k=n)
            for k in range(n):
                product(o[:, k, :], v_q, k, w_q)
            return o

        def result(t0, o, y):
            planes = slice(t0, t0 + o.shape[1])
            nc.vector.tensor_tensor(out=y, in0=o, in1=recalled[:, planes, :], op=ALU.mult)
            nc.sync.dma_start(out=out_planes[:, planes, :], in_=y)

        wm_q = quantise("wm", weave_dealt("wm_woven", wm_raw[:], E))
        memories(0)
        pick_notes(nc.scalar, 0)
        keys = tile("keys", [P, I], U16)[:], tile("keys_sc", [P, I], U8)[:]
        gather(nc.vector, keys[0], key_words, token_list[:])
        gather(nc.vector, keys[1], key_scales, token_list[:])
        memories(1)
        pick_notes(nc.scalar, 1)
        q_q = quantise("q", weave("q_woven", q_raw[:], Q))
        a_sb = [token_scores(h) for h in range(Q // P)]
        pick_notes(nc.vector, 2)
        pick_notes(nc.vector, 3)
        notes_q = quantise("notes", weave_dealt("notes_woven", notes_picked[:], I))
        q2_q = quantise("q2", weave("q2_woven", q2_raw[:], Q))
        recalled = tile("recalled", [P, PACK, Q], F32)
        for t in range(PACK):
            gather(nc.scalar, recalled[:, t, :], memory[t], memory_list[:])
        b_ps = [note_scores(h) for h in range(Q // P)]

        picked = [tile("vals_picked%d" % t, [P, I], BF16) for t in range(2)]
        turned = []
        for t in range(2):
            gather(nc.scalar, picked[t][:], vals_raw[t], token_list[:])
            turned.append(turn_values(picked[t]))
            weigh(t)
        picked.append(late_tile("vals_picked2", [P, I], BF16))
        gather(nc.scalar, picked[2][:], vals_raw[2], token_list[:])
        turned.append(turn_values(picked[2]))
        words01 = late_tile("words01", [P, 2 * Q], F32)
        for t in range(2):
            lay_values(turned[t], words01[:, t * Q : (t + 1) * Q])
        v01 = quantise("v01", words01[:].bitcast(BF16), "codes", 2)
        w_q = quantise("w", weights[:], "codes", 2)
        words2 = late_tile("words2", [P, Q], F32)
        lay_values(turned[2], words2[:])

        picked.append(late_tile("vals_picked3", [P, I], BF16))
        cut = LAST_SHARE // PER_COLUMN
        gather(nc.scalar, picked[3][:, 0:LAST_SHARE], vals_raw[3], token_list[:, 0:cut])
        gather(nc.vector, picked[3][:, LAST_SHARE:I], vals_raw[3], token_list[:, cut : I // PER_COLUMN])
        v2 = quantise("v2", words2[:].bitcast(BF16), "late", LATE_TILES)
        o01 = weighted_values(2, v01)
        turned.append(turn_values(picked[3]))
        y01 = late_tile("y01", [P, 2, Q], F32)
        result(0, o01, y01[:])
        words3 = late_tile("words3", [P, Q], F32)
        lay_values(turned[3], words3[:])
        y_woven = late_tile("y_woven", [P, Q, PACK], BF16)
        nc.scalar.copy(out=y_woven[:, :, 0:2], in_=y01[:].rearrange("p t q -> p q t"))
        v3 = quantise("v3", words3[:].bitcast(BF16), "late", LATE_TILES)
        y23 = late_tile("y23", [P, 2, Q], F32)
        result(2, weighted_values(1, v2), y23[:, 0:1, :])
        result(3, weighted_values(1, v3), y23[:, 1:2, :])
        nc.vector.tensor_copy(out=y_woven[:, :, 2:4], in_=y23[:].rearrange("p t q -> p q t"))

        y_codes, y_scales = quantise("y", y_woven[:].rearrange("p q t -> p (q t)"))
        nc.sync.dma_start(out=out_1[0].rearrange("p n t -> p (n t)").bitcast(I32), in_=y_codes.bitcast(I32))
        for quad in range(P // QUADRANT):
            queue = nc.sync if quad < 2 else nc.scalar
            queue.dma_start(
                out=out_2[0][PACK * quad : PACK * (quad + 1), :].bitcast(I32),
                in_=y_scales[QUADRANT * quad : QUADRANT * quad + PACK, :].bitcast(I32),
            )
